import numpy as np
import ml_dtypes


def mxq(x, axis, fmt="e4m3"):
    dtype, down = {"e4m3": (ml_dtypes.float8_e4m3fn, 7), "e5m2": (ml_dtypes.float8_e5m2, 14)}[fmt]
    v = np.moveaxis(np.asarray(x, np.float32).astype(ml_dtypes.bfloat16).astype(np.float64), axis, -1)
    blocks = v.reshape(v.shape[:-1] + (-1, 32))
    amax = np.abs(blocks).max(-1, keepdims=True)
    byte = np.maximum(np.where(amax > 0, np.frexp(amax)[1] - 1 + 127, 0) - down, 1)
    scale = np.exp2(byte - 127.0)
    codes = (blocks / scale).astype(np.float32).astype(dtype).astype(np.float64)
    return np.moveaxis((codes * scale).reshape(v.shape), -1, axis)


WIDE = False


def mx_kscale(k):
    if not WIDE:
        return np.ones(k)
    levels = np.array([10, -10, 5, -5, 0])
    if k % 512:
        return np.exp2(np.random.permutation(np.resize(levels, k // 32))).repeat(32)
    a = np.empty((k // 512, 16))
    for p in range(k // 512):
        a[p, :8] = np.random.permutation(np.resize(levels, 8))
        for g in range(8):
            far = levels[np.abs(levels - a[p, g]) >= 10]
            a[p, g + 8] = far[np.random.randint(len(far))]
    return np.exp2(a.ravel()).repeat(32)


def f64(x):
    return np.asarray(x).astype(np.float64)


def striped(idx):
    return np.tile(idx.reshape(-1, 16).T, (8, 1)).astype(np.uint16)


def unstriped(offs):
    return offs[:16].T.reshape(-1).astype(np.int64)


def sigmoid(v):
    return 1.0 / (1.0 + np.exp(-np.maximum(v, -700.0)))


K, T, E, C, H, N = 512, 512, 8, 256, 512, 384
TOP = 4


def by_expert(wq, xq):
    return np.concatenate([wq[e].T @ xq[:, e * C:(e + 1) * C] for e in range(E)], axis=1)


def setup_inputs():
    n = np.random.standard_normal
    s = mx_kscale(K)[:, None]
    u = mx_kscale(H)
    deal = np.repeat(np.arange(E), C).reshape(TOP, T)[:, np.random.permutation(T)]
    deal = np.take_along_axis(deal, np.argsort(np.random.rand(TOP, T), axis=0), axis=0)
    for _ in range(8):
        s_, t_ = np.random.permutation(T).reshape(2, -1); r = np.random.randint(TOP, size=T // 2); x, y = deal[r, s_].copy(), deal[r, t_].copy()
        ok = ~((deal[:, s_] == y).any(0) | (deal[:, t_] == x).any(0)); deal[r[ok], s_[ok]] = y[ok]; deal[r[ok], t_[ok]] = x[ok]
    order = np.lexsort((np.random.rand(TOP * T), deal.reshape(-1)))
    slot_token = order % T; pos = np.empty(TOP * T, np.int64); pos[order] = np.arange(TOP * T); pos = pos.reshape(TOP, T)
    g = np.random.uniform(0.5, 1.5, (TOP, T)); g = g / g.sum(0)
    return {
        "xT": (n((K, T)) * s).astype(np.float32),
        "w1": (n((E, K, H)) / np.sqrt(K) / s[None]).astype(np.float32),
        "w3": (n((E, K, H)) / np.sqrt(K) / s[None] * u[None, None, :]).astype(np.float32),
        "w2": (n((E, H, N)) / np.sqrt(H) / u[None, :, None]).astype(np.float32),
        "gate": np.stack([np.tile(r, (N, 1)) for r in g]).astype(np.float32),
        "offs": striped(slot_token),
        "pos1": striped(pos[0]),
        "pos2": striped(pos[1]),
        "pos3": striped(pos[2]),
        "pos4": striped(pos[3]),
    }


def reference(xT, w1, w3, w2, gate, offs, pos1, pos2, pos3, pos4):
    idx = unstriped(offs)
    xq = mxq(f64(xT)[:, idx], 0, "e4m3")
    h = sigmoid(by_expert(mxq(f64(w1), 1, "e4m3"), xq))
    h = h * by_expert(mxq(f64(w3), 1, "e4m3"), xq)
    y = by_expert(mxq(f64(w2), 1, "e4m3"), mxq(h, 0, "e4m3"))
    return sum(f64(gate[r]) * y[:, unstriped(p)] for r, p in enumerate((pos1, pos2, pos3, pos4)))

@@ -1,0 +1,209 @@
+from contextlib import ExitStack
+
+import concourse.mybir as mybir
+
+E, C, T, K, H, N, R = 8, 256, 512, 512, 512, 384, 4
+S = E * C
+FLOPS = 2 * S * (2 * K * H + H * N)
+
+F32 = mybir.dt.float32
+BF16 = mybir.dt.bfloat16
+U32 = mybir.dt.uint32
+U16 = mybir.dt.uint16
+U8 = mybir.dt.uint8
+FP8X4 = mybir.dt.float8_e4m3fn_x4
+SIGMOID = mybir.ActivationFunctionType.Sigmoid
+COPY = mybir.ActivationFunctionType.Copy
+MULT = mybir.AluOpType.mult
+ADD = mybir.AluOpType.add
+
+P = 128
+PACK = 4
+G_BUFS = 3
+NCHUNKS = N // P
+RAW_BUFS = 12
+V_W13 = (16, 64)
+V_W2 = ((1024, 1024), (512, 512), (0, 0))
+V_X = 384
+
+
+def permuted_copy_views(grouped, raw, m0, m1):
+    src = raw[:].rearrange("p j (m t) -> p m j t", t=4)
+    dst = grouped[:].rearrange("p (t m j) -> p m j t", t=4, j=PACK)
+    return dst[:, m0:m1, :, :], src[:, m0:m1, :, :]
+
+
+def plain_copy_views(dst_cols, raw):
+    src = raw.rearrange("p j (c i) -> p c j i", i=4)
+    dst = dst_cols.rearrange("p (c i j) -> p c j i", i=4, j=PACK)
+    return dst, src
+
+
+def tile_moe_tk_glu_sigmoid_kernel(
+    tc, xT, w1, w3, w2, gate, offs, pos1, pos2, pos3, pos4, out
+):
+    nc = tc.nc
+    with ExitStack() as ctx:
+        held = ctx.enter_context(tc.tile_pool(name="held", bufs=1))
+        rawp = ctx.enter_context(tc.tile_pool(name="rawp", bufs=RAW_BUFS))
+        grp = ctx.enter_context(tc.tile_pool(name="grp", bufs=4))
+        gathp = ctx.enter_context(tc.tile_pool(name="gathp", bufs=G_BUFS))
+        codep = ctx.enter_context(tc.tile_pool(name="codep", bufs=4))
+        work = ctx.enter_context(tc.tile_pool(name="work", bufs=4))
+        prodp = ctx.enter_context(tc.tile_pool(name="prodp", bufs=6))
+        psa = ctx.enter_context(tc.psum_pool(name="psa", bufs=3))
+        psg = ctx.enter_context(tc.psum_pool(name="psg", bufs=3))
+        psy = ctx.enter_context(tc.psum_pool(name="psy", bufs=2))
+
+        warm = held.tile([P, 1], F32, name="warm")
+        warm_out = held.tile([P, 1], F32, name="warm_out")
+        nc.vector.memset(warm[:], 0.0)
+        nc.scalar.activation(warm_out[:], warm[:], SIGMOID)
+
+        x_codes = held.tile([P, T], U32, name="x_codes", align_bytes=64)
+        x_scales = held.tile([P, T], U8, name="x_scales", align_bytes=64)
+        nc.gpsimd.memset(x_scales[:], 0)
+
+        x_raw = held.tile([P, PACK, T], F32, name="x_raw")
+        nc.sync.dma_start(out=x_raw[:], in_=xT.rearrange("(p j) t -> p j t", j=PACK))
+        offs_t = held.tile([P, S // 16], U16, name="offs_t")
+        nc.sync.dma_start(offs_t[:], offs)
+
+        raws = {}
+
+        def load_w(q):
+            e = q // 2
+            w = (w1, w3)[q % 2]
+            raw = rawp.tile([P, PACK, H], F32, name="raw")
+            nc.sync.dma_start(out=raw[:], in_=w[e, :, :].rearrange("(p j) h -> p j h", j=PACK))
+            raws[q] = raw
+
+        for q in range(RAW_BUFS):
+            load_w(q)
+
+        pos_t = []
+        for r, pos in enumerate((pos1, pos2, pos3, pos4)):
+            pt = held.tile([P, T // 16], U16, name=f"pos_t{r}")
+            nc.sync.dma_start(pt[:], pos)
+            pos_t.append(pt)
+
+        x_grouped = held.tile([P, T * PACK], BF16, name="x_grouped", align_bytes=64)
+        for t0, t1, on_vector in ((0, V_X, True), (V_X, T, False)):
+            dst, src = plain_copy_views(x_grouped[:, t0 * PACK : t1 * PACK], x_raw[:, :, t0:t1])
+            if on_vector:
+                nc.vector.tensor_copy(out=dst, in_=src)
+            else:
+                nc.scalar.activation(dst, src, COPY)
+        nc.vector.quantize_mx(out=x_codes[:].bitcast(FP8X4), scales=x_scales[:], in_=x_grouped[:])
+
+        y_rows = []
+        for c in range(NCHUNKS):
+            yt = held.tile([P, S], F32, name=f"y_rows{c}")
+            y_rows.append(yt)
+        h_codes, h_scales = [], []
+
+        for e in range(E):
+            cols = slice(e * (C // 16), (e + 1) * (C // 16))
+            g_codes = gathp.tile([P, C], U32, name="g_codes", align_bytes=64)
+            g_scales = gathp.tile([P, C], U8, name="g_scales", align_bytes=64)
+            nc.vector.tensor_copy(g_codes[:], x_codes[:].indirect(offs_t[:, cols]))
+            nc.vector.tensor_copy(g_scales[:], x_scales[:].indirect(offs_t[:, cols]))
+
+            wq = []
+            for i in range(2):
+                raw = raws.pop(2 * e + i)
+                grouped = grp.tile([P, H * PACK], BF16, name="grouped", align_bytes=64)
+                cut = V_W13[i]
+                if cut > 0:
+                    dst, src = permuted_copy_views(grouped, raw, 0, cut)
+                    nc.vector.tensor_copy(out=dst, in_=src)
+                dst, src = permuted_copy_views(grouped, raw, cut, P)
+                nc.scalar.copy(out=dst, in_=src)
+                codes = codep.tile([P, H], U32, name="codes", align_bytes=64)
+                scales = codep.tile([P, H], U8, name="scales", align_bytes=64)
+                nc.vector.quantize_mx(out=codes[:].bitcast(FP8X4), scales=scales[:], in_=grouped[:])
+                wq.append((codes, scales))
+                if 2 * e + i + RAW_BUFS < 2 * E:
+                    load_w(2 * e + i + RAW_BUFS)
+
+            h_grouped = work.tile([P, C, PACK], BF16, name="h_grouped", align_bytes=64)
+            for s in range(C // P):
+                slots = slice(s * P, (s + 1) * P)
+                accs = []
+                for i, pool in enumerate((psa, psg)):
+                    acc = pool.tile([P, PACK, P], F32, name=f"acc{i}")
+                    codes, scales = wq[i]
+                    for t in range(PACK):
+                        nc.tensor.matmul_mx(
+                            out=acc[:, t, :],
+                            lhsT=codes[:, t * P : (t + 1) * P].bitcast(FP8X4),
+                            lhsT_scale=scales[:, t * P : (t + 1) * P],
+                            rhs=g_codes[:, slots].bitcast(FP8X4),
+                            rhs_scale=g_scales[:, slots],
+                            start=True,
+                            stop=True,
+                        )
+                    accs.append(acc)
+                sig = work.tile([P, P, PACK], F32, name="sig")
+                nc.scalar.activation(sig[:], accs[0][:].rearrange("p t s -> p s t"), SIGMOID)
+                nc.vector.tensor_tensor(
+                    h_grouped[:, slots, :], sig[:], accs[1][:].rearrange("p t s -> p s t"), MULT
+                )
+            hc = held.tile([P, C], U32, name=f"h_codes{e}", align_bytes=64)
+            hs = held.tile([P, C], U8, name=f"h_scales{e}", align_bytes=64)
+            nc.vector.quantize_mx(
+                out=hc[:].bitcast(FP8X4), scales=hs[:], in_=h_grouped[:].rearrange("p s t -> p (s t)")
+            )
+            h_codes.append(hc)
+            h_scales.append(hs)
+
+        for c in range(NCHUNKS):
+            n_cols = slice(c * P, (c + 1) * P)
+            raw2 = []
+            for hh in range(2):
+                raw = rawp.tile([P, PACK, 4 * P], F32, name="raw")
+                for q in range(4):
+                    nc.sync.dma_start(
+                        out=raw[:, :, q * P : (q + 1) * P], in_=w2[4 * hh + q, :, n_cols].rearrange("(p j) n -> p j n", j=PACK)
+                    )
+                raw2.append(raw)
+            gt = rawp.tile([P, R, T], F32, name="raw")
+            nc.sync.dma_start(out=gt[:], in_=gate[:, n_cols, :].rearrange("r n t -> n r t"))
+
+            for hh in range(2):
+                grouped = grp.tile([P, H * PACK], BF16, name="grouped", align_bytes=64)
+                cut = V_W2[c][hh] // PACK
+                if cut > 0:
+                    dst, src = plain_copy_views(grouped[:, : cut * PACK], raw2[hh][:, :, :cut])
+                    nc.vector.tensor_copy(out=dst, in_=src)
+                dst, src = plain_copy_views(grouped[:, cut * PACK :], raw2[hh][:, :, cut:])
+                nc.scalar.copy(out=dst, in_=src)
+                codes = codep.tile([P, H], U32, name="codes", align_bytes=64)
+                scales = codep.tile([P, H], U8, name="scales", align_bytes=64)
+                nc.vector.quantize_mx(out=codes[:].bitcast(FP8X4), scales=scales[:], in_=grouped[:])
+                for pair in range(2):
+                    acc = psy.tile([P, 2 * C], F32, name="acc_y")
+                    for q in range(2):
+                        e = 4 * hh + 2 * pair + q
+                        wcols = slice((2 * pair + q) * P, (2 * pair + q + 1) * P)
+                        nc.tensor.matmul_mx(
+                            out=acc[:, q * C : (q + 1) * C],
+                            lhsT=codes[:, wcols].bitcast(FP8X4),
+                            lhsT_scale=scales[:, wcols],
+                            rhs=h_codes[e][:].bitcast(FP8X4),
+                            rhs_scale=h_scales[e][:],
+                            start=True,
+                            stop=True,
+                        )
+                    s0 = (4 * hh + 2 * pair) * C
+                    nc.scalar.copy(out=y_rows[c][:, s0 : s0 + 2 * C], in_=acc[:])
+
+            prods = []
+            for r in range(R):
+                prod = prodp.tile([P, T], F32, name="prod")
+                nc.vector.tensor_tensor(prod[:], y_rows[c][:].indirect(pos_t[r][:]), gt[:, r, :], MULT)
+                prods.append(prod)
+            nc.vector.tensor_tensor(prods[0][:], prods[0][:], prods[1][:], ADD)
+            nc.vector.tensor_tensor(prods[2][:], prods[2][:], prods[3][:], ADD)
+            nc.vector.tensor_tensor(prods[0][:], prods[0][:], prods[2][:], ADD)
+            nc.sync.dma_start(out=out[n_cols, :], in_=prods[0][:])

@@ -19,24 +19,9 @@ ADD = mybir.AluOpType.add
 
 P = 128
 PACK = 4
-G_BUFS = 3
 NCHUNKS = N // P
 RAW_BUFS = 12
-V_W13 = (16, 64)
-V_W2 = ((1024, 1024), (512, 512), (0, 0))
-V_X = 384
-
-
-def permuted_copy_views(grouped, raw, m0, m1):
-    src = raw[:].rearrange("p j (m t) -> p m j t", t=4)
-    dst = grouped[:].rearrange("p (t m j) -> p m j t", t=4, j=PACK)
-    return dst[:, m0:m1, :, :], src[:, m0:m1, :, :]
-
-
-def plain_copy_views(dst_cols, raw):
-    src = raw.rearrange("p j (c i) -> p c j i", i=4)
-    dst = dst_cols.rearrange("p (c i j) -> p c j i", i=4, j=PACK)
-    return dst, src
+X_VECTOR = 384
 
 
 def tile_moe_tk_glu_sigmoid_kernel(
@@ -46,18 +31,17 @@ def tile_moe_tk_glu_sigmoid_kernel(
     with ExitStack() as ctx:
         held = ctx.enter_context(tc.tile_pool(name="held", bufs=1))
         rawp = ctx.enter_context(tc.tile_pool(name="rawp", bufs=RAW_BUFS))
-        grp = ctx.enter_context(tc.tile_pool(name="grp", bufs=4))
-        gathp = ctx.enter_context(tc.tile_pool(name="gathp", bufs=G_BUFS))
-        codep = ctx.enter_context(tc.tile_pool(name="codep", bufs=4))
-        work = ctx.enter_context(tc.tile_pool(name="work", bufs=4))
-        prodp = ctx.enter_context(tc.tile_pool(name="prodp", bufs=6))
+        gathp = ctx.enter_context(tc.tile_pool(name="gathp", bufs=5))
+        grp = ctx.enter_context(tc.tile_pool(name="grp", bufs=5))
+        codep = ctx.enter_context(tc.tile_pool(name="codep", bufs=6))
+        work = ctx.enter_context(tc.tile_pool(name="work", bufs=2))
         psa = ctx.enter_context(tc.psum_pool(name="psa", bufs=3))
         psg = ctx.enter_context(tc.psum_pool(name="psg", bufs=3))
         psy = ctx.enter_context(tc.psum_pool(name="psy", bufs=2))
 
         warm = held.tile([P, 1], F32, name="warm")
         warm_out = held.tile([P, 1], F32, name="warm_out")
-        nc.vector.memset(warm[:], 0.0)
+        nc.gpsimd.memset(warm[:], 0.0)
         nc.scalar.activation(warm_out[:], warm[:], SIGMOID)
 
         x_codes = held.tile([P, T], U32, name="x_codes", align_bytes=64)
@@ -70,16 +54,35 @@ def tile_moe_tk_glu_sigmoid_kernel(
         nc.sync.dma_start(offs_t[:], offs)
 
         raws = {}
+        loads = []
+        for e in range(E):
+            loads += [("w1", e, 0), ("w3", e, 0)]
+        loads += [("w2", 0, 0), ("w2", 0, 1), ("w2", 1, 0), ("w2", 1, 1), ("gate", 0, 0)]
+        loads += [("w2", 2, 0), ("w2", 2, 1), ("gate", 1, 0), ("gate", 2, 0)]
 
-        def load_w(q):
-            e = q // 2
-            w = (w1, w3)[q % 2]
-            raw = rawp.tile([P, PACK, H], F32, name="raw")
-            nc.sync.dma_start(out=raw[:], in_=w[e, :, :].rearrange("(p j) h -> p j h", j=PACK))
-            raws[q] = raw
+        def load_next():
+            if not loads:
+                return
+            kind, i, hh = loads.pop(0)
+            raw = rawp.tile([P, 4, T], F32, name="raw")
+            if kind == "w1":
+                nc.sync.dma_start(out=raw[:], in_=w1[i, :, :].rearrange("(p j) h -> p j h", j=PACK))
+            elif kind == "w3":
+                nc.sync.dma_start(out=raw[:], in_=w3[i, :, :].rearrange("(p j) h -> p j h", j=PACK))
+            elif kind == "w2":
+                for q in range(4):
+                    nc.sync.dma_start(
+                        out=raw[:, q, :].rearrange("p (j n) -> p j n", j=PACK),
+                        in_=w2[4 * hh + q, :, i * P : (i + 1) * P].rearrange("(p j) n -> p j n", j=PACK),
+                    )
+            else:
+                nc.sync.dma_start(
+                    out=raw[:], in_=gate[:, i * P : (i + 1) * P, :].rearrange("r n t -> n r t")
+                )
+            raws[kind, i, hh] = raw
 
         for q in range(RAW_BUFS):
-            load_w(q)
+            load_next()
 
         pos_t = []
         for r, pos in enumerate((pos1, pos2, pos3, pos4)):
@@ -87,52 +90,79 @@ def tile_moe_tk_glu_sigmoid_kernel(
             nc.sync.dma_start(pt[:], pos)
             pos_t.append(pt)
 
-        x_grouped = held.tile([P, T * PACK], BF16, name="x_grouped", align_bytes=64)
-        for t0, t1, on_vector in ((0, V_X, True), (V_X, T, False)):
-            dst, src = plain_copy_views(x_grouped[:, t0 * PACK : t1 * PACK], x_raw[:, :, t0:t1])
+        def plain_copy(on_vector, dst, src):
+            src = src.rearrange("p j (c i) -> p c j i", i=4)
+            dst = dst.rearrange("p (c i j) -> p c j i", i=4, j=PACK)
             if on_vector:
                 nc.vector.tensor_copy(out=dst, in_=src)
             else:
                 nc.scalar.activation(dst, src, COPY)
+
+        x_grouped = held.tile([P, T * PACK], BF16, name="x_grouped", align_bytes=64)
+        for t0, t1, on_vector in ((0, X_VECTOR, True), (X_VECTOR, T, False)):
+            plain_copy(on_vector, x_grouped[:, t0 * PACK : t1 * PACK], x_raw[:, :, t0:t1])
         nc.vector.quantize_mx(out=x_codes[:].bitcast(FP8X4), scales=x_scales[:], in_=x_grouped[:])
 
         y_rows = []
         for c in range(NCHUNKS):
             yt = held.tile([P, S], F32, name=f"y_rows{c}")
             y_rows.append(yt)
-        h_codes, h_scales = [], []
+        weights, gathered, h_codes, w2_codes = {}, {}, {}, {}
+        y_done = []
 
-        for e in range(E):
+        def quantize(grouped):
+            codes = codep.tile([P, H], U32, name="codes", align_bytes=64)
+            scales = codep.tile([P, H], U8, name="scales", align_bytes=64)
+            nc.vector.quantize_mx(out=codes[:].bitcast(FP8X4), scales=scales[:], in_=grouped[:])
+            return codes, scales
+
+        def gather(e):
             cols = slice(e * (C // 16), (e + 1) * (C // 16))
             g_codes = gathp.tile([P, C], U32, name="g_codes", align_bytes=64)
             g_scales = gathp.tile([P, C], U8, name="g_scales", align_bytes=64)
             nc.vector.tensor_copy(g_codes[:], x_codes[:].indirect(offs_t[:, cols]))
             nc.vector.tensor_copy(g_scales[:], x_scales[:].indirect(offs_t[:, cols]))
+            gathered[e] = (g_codes, g_scales)
 
-            wq = []
-            for i in range(2):
-                raw = raws.pop(2 * e + i)
-                grouped = grp.tile([P, H * PACK], BF16, name="grouped", align_bytes=64)
-                cut = V_W13[i]
-                if cut > 0:
-                    dst, src = permuted_copy_views(grouped, raw, 0, cut)
-                    nc.vector.tensor_copy(out=dst, in_=src)
-                dst, src = permuted_copy_views(grouped, raw, cut, P)
+        def prepare(kind, e, vector_halves):
+            raw = raws[kind, e, 0]
+            grouped = grp.tile([P, H * PACK], BF16, name="grouped", align_bytes=64)
+            src = raw[:].rearrange("p j (m t) -> p m j t", t=4)
+            dst = grouped[:].rearrange("p (t m j) -> p m j t", t=4, j=PACK)
+            if len(vector_halves) == 2:
+                nc.vector.tensor_copy(out=dst, in_=src)
+            elif not vector_halves:
                 nc.scalar.copy(out=dst, in_=src)
-                codes = codep.tile([P, H], U32, name="codes", align_bytes=64)
-                scales = codep.tile([P, H], U8, name="scales", align_bytes=64)
-                nc.vector.quantize_mx(out=codes[:].bitcast(FP8X4), scales=scales[:], in_=grouped[:])
-                wq.append((codes, scales))
-                if 2 * e + i + RAW_BUFS < 2 * E:
-                    load_w(2 * e + i + RAW_BUFS)
+            else:
+                for half in range(2):
+                    d, s = dst[:, :, :, 2 * half : 2 * half + 2], src[:, :, :, 2 * half : 2 * half + 2]
+                    if half in vector_halves:
+                        nc.vector.tensor_copy(out=d, in_=s)
+                    else:
+                        nc.scalar.copy(out=d, in_=s)
+            weights[kind, e] = quantize(grouped)
 
+        def prepare_w2(c, hh, on_vector):
+            raw = raws["w2", c, hh]
+            grouped = grp.tile([P, H * PACK], BF16, name="grouped", align_bytes=64)
+            for q in range(4):
+                plain_copy(
+                    q < on_vector,
+                    grouped[:, q * 512 : (q + 1) * 512],
+                    raw[:, q, :].rearrange("p (j n) -> p j n", j=PACK),
+                )
+            w2_codes[c, hh] = quantize(grouped)
+
+        def first_layer(e):
+            g_codes, g_scales = gathered.pop(e)
+            host = raws["w1", min(e + 1, E - 1), 0]
             h_grouped = work.tile([P, C, PACK], BF16, name="h_grouped", align_bytes=64)
             for s in range(C // P):
                 slots = slice(s * P, (s + 1) * P)
                 accs = []
-                for i, pool in enumerate((psa, psg)):
-                    acc = pool.tile([P, PACK, P], F32, name=f"acc{i}")
-                    codes, scales = wq[i]
+                for kind, pool in (("w1", psa), ("w3", psg)):
+                    acc = pool.tile([P, PACK, P], F32, name=f"acc_{kind}")
+                    codes, scales = weights[kind, e]
                     for t in range(PACK):
                         nc.tensor.matmul_mx(
                             out=acc[:, t, :],
@@ -143,67 +173,69 @@ def tile_moe_tk_glu_sigmoid_kernel(
                             start=True,
                             stop=True,
                         )
-                    accs.append(acc)
-                sig = work.tile([P, P, PACK], F32, name="sig")
-                nc.scalar.activation(sig[:], accs[0][:].rearrange("p t s -> p s t"), SIGMOID)
-                nc.vector.tensor_tensor(
-                    h_grouped[:, slots, :], sig[:], accs[1][:].rearrange("p t s -> p s t"), MULT
-                )
+                    accs.append(acc[:].rearrange("p t s -> p s t"))
+                sig = host[:, s + (2 if e == E - 1 else 0), :].rearrange("p (s t) -> p s t", t=PACK)
+                nc.scalar.activation(sig, accs[0], SIGMOID)
+                nc.vector.tensor_tensor(h_grouped[:, slots, :], sig, accs[1], MULT)
             hc = held.tile([P, C], U32, name=f"h_codes{e}", align_bytes=64)
             hs = held.tile([P, C], U8, name=f"h_scales{e}", align_bytes=64)
             nc.vector.quantize_mx(
                 out=hc[:].bitcast(FP8X4), scales=hs[:], in_=h_grouped[:].rearrange("p s t -> p (s t)")
             )
-            h_codes.append(hc)
-            h_scales.append(hs)
+            h_codes[e] = (hc, hs)
 
-        for c in range(NCHUNKS):
-            n_cols = slice(c * P, (c + 1) * P)
-            raw2 = []
-            for hh in range(2):
-                raw = rawp.tile([P, PACK, 4 * P], F32, name="raw")
-                for q in range(4):
-                    nc.sync.dma_start(
-                        out=raw[:, :, q * P : (q + 1) * P], in_=w2[4 * hh + q, :, n_cols].rearrange("(p j) n -> p j n", j=PACK)
-                    )
-                raw2.append(raw)
-            gt = rawp.tile([P, R, T], F32, name="raw")
-            nc.sync.dma_start(out=gt[:], in_=gate[:, n_cols, :].rearrange("r n t -> n r t"))
-
-            for hh in range(2):
-                grouped = grp.tile([P, H * PACK], BF16, name="grouped", align_bytes=64)
-                cut = V_W2[c][hh] // PACK
-                if cut > 0:
-                    dst, src = plain_copy_views(grouped[:, : cut * PACK], raw2[hh][:, :, :cut])
-                    nc.vector.tensor_copy(out=dst, in_=src)
-                dst, src = plain_copy_views(grouped[:, cut * PACK :], raw2[hh][:, :, cut:])
-                nc.scalar.copy(out=dst, in_=src)
-                codes = codep.tile([P, H], U32, name="codes", align_bytes=64)
-                scales = codep.tile([P, H], U8, name="scales", align_bytes=64)
-                nc.vector.quantize_mx(out=codes[:].bitcast(FP8X4), scales=scales[:], in_=grouped[:])
-                for pair in range(2):
+        def second_layer():
+            for c in range(NCHUNKS):
+                for pair in range(E // 2):
+                    if (c, pair) in y_done or (c, pair // 2) not in w2_codes or 2 * pair + 1 not in h_codes:
+                        continue
+                    y_done.append((c, pair))
+                    codes, scales = w2_codes[c, pair // 2]
                     acc = psy.tile([P, 2 * C], F32, name="acc_y")
                     for q in range(2):
-                        e = 4 * hh + 2 * pair + q
-                        wcols = slice((2 * pair + q) * P, (2 * pair + q + 1) * P)
+                        e = 2 * pair + q
+                        wcols = slice((e % 4) * P, (e % 4 + 1) * P)
+                        hc, hs = h_codes[e]
                         nc.tensor.matmul_mx(
                             out=acc[:, q * C : (q + 1) * C],
                             lhsT=codes[:, wcols].bitcast(FP8X4),
                             lhsT_scale=scales[:, wcols],
-                            rhs=h_codes[e][:].bitcast(FP8X4),
-                            rhs_scale=h_scales[e][:],
+                            rhs=hc[:].bitcast(FP8X4),
+                            rhs_scale=hs[:],
                             start=True,
                             stop=True,
                         )
-                    s0 = (4 * hh + 2 * pair) * C
-                    nc.scalar.copy(out=y_rows[c][:, s0 : s0 + 2 * C], in_=acc[:])
+                    nc.scalar.copy(out=y_rows[c][:, 2 * pair * C : 2 * (pair + 1) * C], in_=acc[:])
 
-            prods = []
+        def combine(c, prods):
+            gates = raws["gate", c, 0]
             for r in range(R):
-                prod = prodp.tile([P, T], F32, name="prod")
-                nc.vector.tensor_tensor(prod[:], y_rows[c][:].indirect(pos_t[r][:]), gt[:, r, :], MULT)
-                prods.append(prod)
-            nc.vector.tensor_tensor(prods[0][:], prods[0][:], prods[1][:], ADD)
-            nc.vector.tensor_tensor(prods[2][:], prods[2][:], prods[3][:], ADD)
-            nc.vector.tensor_tensor(prods[0][:], prods[0][:], prods[2][:], ADD)
-            nc.sync.dma_start(out=out[n_cols, :], in_=prods[0][:])
+                nc.vector.tensor_tensor(prods[:, r, :], y_rows[c][:].indirect(pos_t[r][:]), gates[:, r, :], MULT)
+            nc.vector.tensor_tensor(prods[:, 0:2, :], prods[:, 0:2, :], prods[:, 2:4, :], ADD)
+            nc.vector.tensor_tensor(prods[:, 0, :], prods[:, 0, :], prods[:, 1, :], ADD)
+            nc.sync.dma_start(out=out[c * P : (c + 1) * P, :], in_=prods[:, 0, :])
+
+        for e in range(E):
+            gather(e)
+            prepare("w1", e, ())
+            if e == 0:
+                load_next()
+            prepare("w3", e, (0, 1) if e >= 4 else (0,))
+            load_next()
+            if e > 0:
+                first_layer(e - 1)
+                load_next()
+        first_layer(E - 1)
+        load_next()
+
+        V2 = (2, 0, 0)
+        for c in range(NCHUNKS):
+            for hh in range(2):
+                prepare_w2(c, hh, V2[c])
+                second_layer()
+                if c != 1:
+                    load_next()
+        combine(0, raws["w2", 1, 0])
+        combine(1, raws["w2", 1, 1])
+        prods = held.tile([P, R, T], F32, name="prods")
+        combine(2, prods)

@@ -21,7 +21,6 @@ P = 128
 PACK = 4
 NCHUNKS = N // P
 RAW_BUFS = 12
-X_VECTOR = 384
 
 
 def tile_moe_tk_glu_sigmoid_kernel(
@@ -31,9 +30,9 @@ def tile_moe_tk_glu_sigmoid_kernel(
     with ExitStack() as ctx:
         held = ctx.enter_context(tc.tile_pool(name="held", bufs=1))
         rawp = ctx.enter_context(tc.tile_pool(name="rawp", bufs=RAW_BUFS))
-        gathp = ctx.enter_context(tc.tile_pool(name="gathp", bufs=5))
-        grp = ctx.enter_context(tc.tile_pool(name="grp", bufs=5))
+        grp = ctx.enter_context(tc.tile_pool(name="grp", bufs=6))
         codep = ctx.enter_context(tc.tile_pool(name="codep", bufs=6))
+        prodp = ctx.enter_context(tc.tile_pool(name="prodp", bufs=2))
         work = ctx.enter_context(tc.tile_pool(name="work", bufs=2))
         psa = ctx.enter_context(tc.psum_pool(name="psa", bufs=3))
         psg = ctx.enter_context(tc.psum_pool(name="psg", bufs=3))
@@ -99,8 +98,7 @@ def tile_moe_tk_glu_sigmoid_kernel(
                 nc.scalar.activation(dst, src, COPY)
 
         x_grouped = held.tile([P, T * PACK], BF16, name="x_grouped", align_bytes=64)
-        for t0, t1, on_vector in ((0, X_VECTOR, True), (X_VECTOR, T, False)):
-            plain_copy(on_vector, x_grouped[:, t0 * PACK : t1 * PACK], x_raw[:, :, t0:t1])
+        plain_copy(True, x_grouped[:], x_raw[:])
         nc.vector.quantize_mx(out=x_codes[:].bitcast(FP8X4), scales=x_scales[:], in_=x_grouped[:])
 
         y_rows = []
@@ -118,8 +116,8 @@ def tile_moe_tk_glu_sigmoid_kernel(
 
         def gather(e):
             cols = slice(e * (C // 16), (e + 1) * (C // 16))
-            g_codes = gathp.tile([P, C], U32, name="g_codes", align_bytes=64)
-            g_scales = gathp.tile([P, C], U8, name="g_scales", align_bytes=64)
+            g_codes = held.tile([P, C], U32, name=f"g_codes{e}", align_bytes=64)
+            g_scales = held.tile([P, C], U8, name=f"g_scales{e}", align_bytes=64)
             nc.vector.tensor_copy(g_codes[:], x_codes[:].indirect(offs_t[:, cols]))
             nc.vector.tensor_copy(g_scales[:], x_scales[:].indirect(offs_t[:, cols]))
             gathered[e] = (g_codes, g_scales)
@@ -207,20 +205,30 @@ def tile_moe_tk_glu_sigmoid_kernel(
                         )
                     nc.scalar.copy(out=y_rows[c][:, 2 * pair * C : 2 * (pair + 1) * C], in_=acc[:])
 
-        def combine(c, prods):
+        def combine(c):
             gates = raws["gate", c, 0]
+            prods = prodp.tile([P, R, T], F32, name="prods")
             for r in range(R):
                 nc.vector.tensor_tensor(prods[:, r, :], y_rows[c][:].indirect(pos_t[r][:]), gates[:, r, :], MULT)
-            nc.vector.tensor_tensor(prods[:, 0:2, :], prods[:, 0:2, :], prods[:, 2:4, :], ADD)
-            nc.vector.tensor_tensor(prods[:, 0, :], prods[:, 0, :], prods[:, 1, :], ADD)
-            nc.sync.dma_start(out=out[c * P : (c + 1) * P, :], in_=prods[:, 0, :])
+            rows = out[c * P : (c + 1) * P, :]
+            if c < NCHUNKS - 1:
+                nc.vector.tensor_tensor(prods[:, 0:2, :], prods[:, 0:2, :], prods[:, 2:4, :], ADD)
+                nc.vector.tensor_tensor(prods[:, 0, :], prods[:, 0, :], prods[:, 1, :], ADD)
+                nc.sync.dma_start(out=rows, in_=prods[:, 0, :])
+            else:
+                nc.vector.tensor_tensor(prods[:, 0, :], prods[:, 0, :], prods[:, 1, :], ADD)
+                nc.vector.tensor_tensor(prods[:, 2, :], prods[:, 2, :], prods[:, 3, :], ADD)
+                for half in range(2):
+                    cols = slice(half * (T // 2), (half + 1) * (T // 2))
+                    nc.vector.tensor_tensor(prods[:, 0, cols], prods[:, 0, cols], prods[:, 2, cols], ADD)
+                    nc.sync.dma_start(out=rows[:, cols], in_=prods[:, 0, cols])
 
         for e in range(E):
             gather(e)
-            prepare("w1", e, ())
+            prepare("w1", e, (0,) if e in (2, 3) else ())
             if e == 0:
                 load_next()
-            prepare("w3", e, (0, 1) if e >= 4 else (0,))
+            prepare("w3", e, (0, 1) if e >= 4 else (0,) if e >= 2 else ())
             load_next()
             if e > 0:
                 first_layer(e - 1)
@@ -228,14 +236,12 @@ def tile_moe_tk_glu_sigmoid_kernel(
         first_layer(E - 1)
         load_next()
 
-        V2 = (2, 0, 0)
+        V2 = {(0, 0): 2, (0, 1): 1, (1, 0): 4, (1, 1): 4, (2, 1): 1}
         for c in range(NCHUNKS):
             for hh in range(2):
-                prepare_w2(c, hh, V2[c])
+                prepare_w2(c, hh, V2.get((c, hh), 0))
+                load_next()
                 second_layer()
-                if c != 1:
-                    load_next()
-        combine(0, raws["w2", 1, 0])
-        combine(1, raws["w2", 1, 1])
-        prods = held.tile([P, R, T], F32, name="prods")
-        combine(2, prods)
+            if c > 0:
+                combine(c - 1)
+        combine(NCHUNKS - 1)

from contextlib import ExitStack

import concourse.mybir as mybir

E, C, T, K, H, N, R = 8, 256, 512, 512, 512, 384, 4
S = E * C
FLOPS = 2 * S * (2 * K * H + H * N)

F32 = mybir.dt.float32
BF16 = mybir.dt.bfloat16
U32 = mybir.dt.uint32
U16 = mybir.dt.uint16
U8 = mybir.dt.uint8
FP8X4 = mybir.dt.float8_e4m3fn_x4
SIGMOID = mybir.ActivationFunctionType.Sigmoid
COPY = mybir.ActivationFunctionType.Copy
MULT = mybir.AluOpType.mult
ADD = mybir.AluOpType.add

P = 128
PACK = 4
NCHUNKS = N // P
RAW_BUFS = 12


def tile_moe_tk_glu_sigmoid_kernel(
    tc, xT, w1, w3, w2, gate, offs, pos1, pos2, pos3, pos4, out
):
    nc = tc.nc
    with ExitStack() as ctx:
        held = ctx.enter_context(tc.tile_pool(name="held", bufs=1))
        rawp = ctx.enter_context(tc.tile_pool(name="rawp", bufs=RAW_BUFS))
        grp = ctx.enter_context(tc.tile_pool(name="grp", bufs=6))
        codep = ctx.enter_context(tc.tile_pool(name="codep", bufs=6))
        prodp = ctx.enter_context(tc.tile_pool(name="prodp", bufs=2))
        work = ctx.enter_context(tc.tile_pool(name="work", bufs=2))
        psa = ctx.enter_context(tc.psum_pool(name="psa", bufs=3))
        psg = ctx.enter_context(tc.psum_pool(name="psg", bufs=3))
        psy = ctx.enter_context(tc.psum_pool(name="psy", bufs=2))

        warm = held.tile([P, 1], F32, name="warm")
        warm_out = held.tile([P, 1], F32, name="warm_out")
        nc.gpsimd.memset(warm[:], 0.0)
        nc.scalar.activation(warm_out[:], warm[:], SIGMOID)

        x_codes = held.tile([P, T], U32, name="x_codes", align_bytes=64)
        x_scales = held.tile([P, T], U8, name="x_scales", align_bytes=64)
        nc.gpsimd.memset(x_scales[:], 0)

        x_raw = held.tile([P, PACK, T], F32, name="x_raw")
        nc.sync.dma_start(out=x_raw[:], in_=xT.rearrange("(p j) t -> p j t", j=PACK))
        offs_t = held.tile([P, S // 16], U16, name="offs_t")
        nc.sync.dma_start(offs_t[:], offs)

        raws = {}
        loads = []
        for e in range(E):
            loads += [("w1", e, 0), ("w3", e, 0)]
        loads += [("w2", 0, 0), ("w2", 0, 1), ("w2", 1, 0), ("w2", 1, 1), ("gate", 0, 0)]
        loads += [("w2", 2, 0), ("w2", 2, 1), ("gate", 1, 0), ("gate", 2, 0)]

        def load_next():
            if not loads:
                return
            kind, i, hh = loads.pop(0)
            raw = rawp.tile([P, 4, T], F32, name="raw")
            if kind == "w1":
                nc.sync.dma_start(out=raw[:], in_=w1[i, :, :].rearrange("(p j) h -> p j h", j=PACK))
            elif kind == "w3":
                nc.sync.dma_start(out=raw[:], in_=w3[i, :, :].rearrange("(p j) h -> p j h", j=PACK))
            elif kind == "w2":
                for q in range(4):
                    nc.sync.dma_start(
                        out=raw[:, q, :].rearrange("p (j n) -> p j n", j=PACK),
                        in_=w2[4 * hh + q, :, i * P : (i + 1) * P].rearrange("(p j) n -> p j n", j=PACK),
                    )
            else:
                nc.sync.dma_start(
                    out=raw[:], in_=gate[:, i * P : (i + 1) * P, :].rearrange("r n t -> n r t")
                )
            raws[kind, i, hh] = raw

        for q in range(RAW_BUFS):
            load_next()

        pos_t = []
        for r, pos in enumerate((pos1, pos2, pos3, pos4)):
            pt = held.tile([P, T // 16], U16, name=f"pos_t{r}")
            nc.sync.dma_start(pt[:], pos)
            pos_t.append(pt)

        def plain_copy(on_vector, dst, src):
            src = src.rearrange("p j (c i) -> p c j i", i=4)
            dst = dst.rearrange("p (c i j) -> p c j i", i=4, j=PACK)
            if on_vector:
                nc.vector.tensor_copy(out=dst, in_=src)
            else:
                nc.scalar.activation(dst, src, COPY)

        x_grouped = held.tile([P, T * PACK], BF16, name="x_grouped", align_bytes=64)
        plain_copy(True, x_grouped[:], x_raw[:])
        nc.vector.quantize_mx(out=x_codes[:].bitcast(FP8X4), scales=x_scales[:], in_=x_grouped[:])

        y_rows = []
        for c in range(NCHUNKS):
            yt = held.tile([P, S], F32, name=f"y_rows{c}")
            y_rows.append(yt)
        weights, gathered, h_codes, w2_codes = {}, {}, {}, {}
        y_done = []

        def quantize(grouped):
            codes = codep.tile([P, H], U32, name="codes", align_bytes=64)
            scales = codep.tile([P, H], U8, name="scales", align_bytes=64)
            nc.vector.quantize_mx(out=codes[:].bitcast(FP8X4), scales=scales[:], in_=grouped[:])
            return codes, scales

        def gather(e):
            cols = slice(e * (C // 16), (e + 1) * (C // 16))
            g_codes = held.tile([P, C], U32, name=f"g_codes{e}", align_bytes=64)
            g_scales = held.tile([P, C], U8, name=f"g_scales{e}", align_bytes=64)
            nc.vector.tensor_copy(g_codes[:], x_codes[:].indirect(offs_t[:, cols]))
            nc.vector.tensor_copy(g_scales[:], x_scales[:].indirect(offs_t[:, cols]))
            gathered[e] = (g_codes, g_scales)

        def prepare(kind, e, vector_halves):
            raw = raws[kind, e, 0]
            grouped = grp.tile([P, H * PACK], BF16, name="grouped", align_bytes=64)
            src = raw[:].rearrange("p j (m t) -> p m j t", t=4)
            dst = grouped[:].rearrange("p (t m j) -> p m j t", t=4, j=PACK)
            if len(vector_halves) == 2:
                nc.vector.tensor_copy(out=dst, in_=src)
            elif not vector_halves:
                nc.scalar.copy(out=dst, in_=src)
            else:
                for half in range(2):
                    d, s = dst[:, :, :, 2 * half : 2 * half + 2], src[:, :, :, 2 * half : 2 * half + 2]
                    if half in vector_halves:
                        nc.vector.tensor_copy(out=d, in_=s)
                    else:
                        nc.scalar.copy(out=d, in_=s)
            weights[kind, e] = quantize(grouped)

        def prepare_w2(c, hh, on_vector):
            raw = raws["w2", c, hh]
            grouped = grp.tile([P, H * PACK], BF16, name="grouped", align_bytes=64)
            for q in range(4):
                plain_copy(
                    q < on_vector,
                    grouped[:, q * 512 : (q + 1) * 512],
                    raw[:, q, :].rearrange("p (j n) -> p j n", j=PACK),
                )
            w2_codes[c, hh] = quantize(grouped)

        def first_layer(e):
            g_codes, g_scales = gathered.pop(e)
            host = raws["w1", min(e + 1, E - 1), 0]
            h_grouped = work.tile([P, C, PACK], BF16, name="h_grouped", align_bytes=64)
            for s in range(C // P):
                slots = slice(s * P, (s + 1) * P)
                accs = []
                for kind, pool in (("w1", psa), ("w3", psg)):
                    acc = pool.tile([P, PACK, P], F32, name=f"acc_{kind}")
                    codes, scales = weights[kind, e]
                    for t in range(PACK):
                        nc.tensor.matmul_mx(
                            out=acc[:, t, :],
                            lhsT=codes[:, t * P : (t + 1) * P].bitcast(FP8X4),
                            lhsT_scale=scales[:, t * P : (t + 1) * P],
                            rhs=g_codes[:, slots].bitcast(FP8X4),
                            rhs_scale=g_scales[:, slots],
                            start=True,
                            stop=True,
                        )
                    accs.append(acc[:].rearrange("p t s -> p s t"))
                sig = host[:, s + (2 if e == E - 1 else 0), :].rearrange("p (s t) -> p s t", t=PACK)
                nc.scalar.activation(sig, accs[0], SIGMOID)
                nc.vector.tensor_tensor(h_grouped[:, slots, :], sig, accs[1], MULT)
            hc = held.tile([P, C], U32, name=f"h_codes{e}", align_bytes=64)
            hs = held.tile([P, C], U8, name=f"h_scales{e}", align_bytes=64)
            nc.vector.quantize_mx(
                out=hc[:].bitcast(FP8X4), scales=hs[:], in_=h_grouped[:].rearrange("p s t -> p (s t)")
            )
            h_codes[e] = (hc, hs)

        def second_layer():
            for c in range(NCHUNKS):
                for pair in range(E // 2):
                    if (c, pair) in y_done or (c, pair // 2) not in w2_codes or 2 * pair + 1 not in h_codes:
                        continue
                    y_done.append((c, pair))
                    codes, scales = w2_codes[c, pair // 2]
                    acc = psy.tile([P, 2 * C], F32, name="acc_y")
                    for q in range(2):
                        e = 2 * pair + q
                        wcols = slice((e % 4) * P, (e % 4 + 1) * P)
                        hc, hs = h_codes[e]
                        nc.tensor.matmul_mx(
                            out=acc[:, q * C : (q + 1) * C],
                            lhsT=codes[:, wcols].bitcast(FP8X4),
                            lhsT_scale=scales[:, wcols],
                            rhs=hc[:].bitcast(FP8X4),
                            rhs_scale=hs[:],
                            start=True,
                            stop=True,
                        )
                    nc.scalar.copy(out=y_rows[c][:, 2 * pair * C : 2 * (pair + 1) * C], in_=acc[:])

        def combine(c):
            gates = raws["gate", c, 0]
            prods = prodp.tile([P, R, T], F32, name="prods")
            for r in range(R):
                nc.vector.tensor_tensor(prods[:, r, :], y_rows[c][:].indirect(pos_t[r][:]), gates[:, r, :], MULT)
            rows = out[c * P : (c + 1) * P, :]
            if c < NCHUNKS - 1:
                nc.vector.tensor_tensor(prods[:, 0:2, :], prods[:, 0:2, :], prods[:, 2:4, :], ADD)
                nc.vector.tensor_tensor(prods[:, 0, :], prods[:, 0, :], prods[:, 1, :], ADD)
                nc.sync.dma_start(out=rows, in_=prods[:, 0, :])
            else:
                nc.vector.tensor_tensor(prods[:, 0, :], prods[:, 0, :], prods[:, 1, :], ADD)
                nc.vector.tensor_tensor(prods[:, 2, :], prods[:, 2, :], prods[:, 3, :], ADD)
                for half in range(2):
                    cols = slice(half * (T // 2), (half + 1) * (T // 2))
                    nc.vector.tensor_tensor(prods[:, 0, cols], prods[:, 0, cols], prods[:, 2, cols], ADD)
                    nc.sync.dma_start(out=rows[:, cols], in_=prods[:, 0, cols])

        for e in range(E):
            gather(e)
            prepare("w1", e, (0,) if e in (2, 3) else ())
            if e == 0:
                load_next()
            prepare("w3", e, (0, 1) if e >= 4 else (0,) if e >= 2 else ())
            load_next()
            if e > 0:
                first_layer(e - 1)
                load_next()
        first_layer(E - 1)
        load_next()

        V2 = {(0, 0): 2, (0, 1): 1, (1, 0): 4, (1, 1): 4, (2, 1): 1}
        for c in range(NCHUNKS):
            for hh in range(2):
                prepare_w2(c, hh, V2.get((c, hh), 0))
                load_next()
                second_layer()
            if c > 0:
                combine(c - 1)
        combine(NCHUNKS - 1)
